import numpy as np
import ml_dtypes


def mxq(x, axis, fmt="e4m3"):
    dtype, down = {"e4m3": (ml_dtypes.float8_e4m3fn, 7), "e5m2": (ml_dtypes.float8_e5m2, 14)}[fmt]
    v = np.moveaxis(np.asarray(x, np.float32).astype(ml_dtypes.bfloat16).astype(np.float64), axis, -1)
    blocks = v.reshape(v.shape[:-1] + (-1, 32))
    amax = np.abs(blocks).max(-1, keepdims=True)
    byte = np.maximum(np.where(amax > 0, np.frexp(amax)[1] - 1 + 127, 0) - down, 1)
    scale = np.exp2(byte - 127.0)
    codes = (blocks / scale).astype(np.float32).astype(dtype).astype(np.float64)
    return np.moveaxis((codes * scale).reshape(v.shape), -1, axis)


WIDE = False


def mx_kscale(k):
    if not WIDE:
        return np.ones(k)
    levels = np.array([10, -10, 5, -5, 0])
    if k % 512:
        return np.exp2(np.random.permutation(np.resize(levels, k // 32))).repeat(32)
    a = np.empty((k // 512, 16))
    for p in range(k // 512):
        a[p, :8] = np.random.permutation(np.resize(levels, 8))
        for g in range(8):
            far = levels[np.abs(levels - a[p, g]) >= 10]
            a[p, g + 8] = far[np.random.randint(len(far))]
    return np.exp2(a.ravel()).repeat(32)


def f64(x):
    return np.asarray(x).astype(np.float64)


def striped8(idx):
    return np.concatenate([x.reshape(-1, 16).T for x in idx]).astype(np.uint16)


def runs(offs, k):
    lists = np.stack([offs[16 * r : 16 * r + 16].T.reshape(-1) for r in range(8)]).astype(np.int64)
    return lists[np.arange(k) % 512 // 64]


def pack_weight(w):
    k, n = w.shape
    w = f64(np.asarray(w, np.float32).astype(ml_dtypes.bfloat16)).reshape(k // 32, 32, n)
    amax = np.abs(w).max(1)
    byte = np.clip(np.where(amax > 0, np.frexp(amax)[1] - 1 + 127 - 7, 1), 1, 254)
    scaled = (w * np.exp2(127.0 - byte)[:, None, :]).reshape(k, n).astype(np.float32)
    words = np.ascontiguousarray(scaled.reshape(k // 512, 128, 4, n).transpose(0, 1, 3, 2)).astype(ml_dtypes.float8_e4m3fn).view(np.uint8)
    return words, np.ascontiguousarray(byte.astype(np.uint8).reshape(k // 512, 16, n))


def unpack_weight(words, scales):
    g, p, n, _ = words.shape
    vals = np.ascontiguousarray(words).view(ml_dtypes.float8_e4m3fn).astype(np.float64) * np.repeat(np.exp2(scales.astype(np.float64) - 127.0), 8, axis=1)[..., None]
    return vals.transpose(0, 1, 3, 2).reshape(g * 512, n)

def planes(y):
    n, m = y.shape
    v = y.astype(np.float32).astype(ml_dtypes.bfloat16).astype(np.float64).reshape(n // 32, 32, m)
    top = np.abs(v).max(1)
    byte = np.clip(np.where(top > 0, np.frexp(top)[1] - 1 + 127 - 7, 1), 1, 254)
    codes = (v * np.exp2(127.0 - byte)[:, None, :]).reshape(n, m).astype(np.float32).astype(ml_dtypes.float8_e4m3fn).view(np.uint8)
    words = codes.reshape(n // 512, 128, 4, m).transpose(0, 1, 3, 2)
    return np.ascontiguousarray(words), np.ascontiguousarray(byte.astype(np.uint8).reshape(n // 512, 16, m))


K, T, S, N, H = 512, 2048, 512, 512, 512


def setup_inputs():
    n = np.random.standard_normal
    s = mx_kscale(K)[:, None]
    u = mx_kscale(H)
    packed_xT = pack_weight(n((K, T)) * s)
    packed_w1 = pack_weight(n((K, H)) / np.sqrt(K) / s)
    packed_w2 = pack_weight(n((H, N)) / np.sqrt(H) / u[:, None])
    return {
        "x_words": packed_xT[0],
        "x_scales": packed_xT[1],
        "w1_words": packed_w1[0],
        "w1_scales": packed_w1[1],
        "gn": (np.random.uniform(0.5, 1.5, (H, 1)) * u[:, None]).astype(np.float32),
        "w2_words": packed_w2[0],
        "w2_scales": packed_w2[1],
        "offs": striped8(np.random.randint(0, T, (8, S))),
        "n1": striped8(np.stack([np.random.permutation(S) for _ in range(8)])),
        "n2": striped8(np.stack([np.random.permutation(S) for _ in range(8)])),
        "n3": striped8(np.stack([np.random.permutation(S) for _ in range(8)])),
    }


def reference(x_words, x_scales, w1_words, w1_scales, gn, w2_words, w2_scales, offs, n1, n2, n3):
    xq = unpack_weight(x_words, x_scales)[np.arange(K)[:, None], runs(offs, K)]
    y = unpack_weight(w1_words, w1_scales).T @ xq
    st = y - (y[np.arange(H)[:, None], runs(n1, H)])
    z = f64(gn) * (st - (0.5 * (st[np.arange(H)[:, None], runs(n1, H)])))
    h = unpack_weight(w2_words, w2_scales).T @ mxq(z, 0, "e4m3")
    pa = h[np.arange(N)[:, None], runs(n2, N)]
    pb = h[np.arange(N)[:, None], runs(n3, N)]
    out_0 = np.maximum(np.minimum(h, pa), np.minimum(np.maximum(h, pa), pb))
    return (out_0,) + planes(out_0)

@@ -1,0 +1,222 @@
+from contextlib import ExitStack
+
+import concourse.mybir as mybir
+
+K, T, S, N, H = 512, 2048, 512, 512, 512
+FLOPS = 2 * K * H * S + 2 * H * N * S
+
+F32 = mybir.dt.float32
+BF16 = mybir.dt.bfloat16
+I32 = mybir.dt.int32
+U32 = mybir.dt.uint32
+U16 = mybir.dt.uint16
+U8 = mybir.dt.uint8
+FP8X4 = mybir.dt.float8_e4m3fn_x4
+ALU = mybir.AluOpType
+COPY = mybir.ActivationFunctionType.Copy
+
+P = 128
+PACK = 4
+GROUP = 16
+HALF = S // 2
+Z_PIECES = ((0, 256), (256, 384), (384, 512))
+OUT_PIECES = ((0, 256), (256, 384), (384, 512))
+
+
+def tile_picked_hashtwicemed_none_po_kernel(
+    tc, x_words, x_scales, w1_words, w1_scales, gn, w2_words, w2_scales, offs, n1, n2, n3, out_0, out_1, out_2
+):
+    nc = tc.nc
+
+    def words_of(dram):
+        return dram[0].rearrange("p n t -> p (n t)").bitcast(I32)
+
+    def cut(lists, lo, hi):
+        return lists[:, lo // GROUP : hi // GROUP]
+
+    with ExitStack() as ctx:
+        sb = ctx.enter_context(tc.tile_pool(name="sb", bufs=1))
+        ps = ctx.enter_context(tc.psum_pool(name="ps", bufs=1))
+
+        def tile(name, shape, dtype):
+            return sb.tile(shape, dtype, name=name, align_bytes=64)
+
+        offs_t = tile("offs_t", [P, S // GROUP], U16)
+        n1_t = tile("n1_t", [P, S // GROUP], U16)
+        n2_t = tile("n2_t", [P, S // GROUP], U16)
+        n3_t = tile("n3_t", [P, S // GROUP], U16)
+        xw = tile("xw", [P, T], U32)
+        xs = tile("xs", [P, T], U8)
+        w1w = tile("w1w", [P, H], I32)
+        w2w = tile("w2w", [P, N], I32)
+        w1s = tile("w1s", [P, H], U8)
+        w2s = tile("w2s", [P, N], U8)
+        gain = tile("gain", [P, PACK], F32)
+        warm = tile("warm", [P, 8], F32)
+        warm2 = tile("warm2", [P, 8], F32)
+
+        nc.vector.memset(warm[:], 0.0)
+
+        def load_scales(queue, dst, src):
+            for q in range(4):
+                rows = src[0, 4 * q : 4 * q + 4, :].bitcast(I32)
+                queue.dma_start(dst[32 * q : 32 * q + 32, :].bitcast(I32), rows.partition_broadcast(8))
+
+        nc.sync.dma_start(offs_t[:], offs)
+        nc.sync.dma_start(xs[:].bitcast(I32), x_scales[0].bitcast(I32).unsqueeze(1).to_broadcast([16, 8, T // 4]))
+        load_scales(nc.sync, w1s, w1_scales)
+        nc.sync.dma_start(w1w[:], words_of(w1_words))
+        nc.sync.dma_start(xw[:].bitcast(I32), words_of(x_words))
+        nc.sync.dma_start(n1_t[:], n1)
+        nc.sync.dma_start(n2_t[:], n2)
+        nc.sync.dma_start(n3_t[:], n3)
+        nc.sync.dma_start(w2w[:], words_of(w2_words))
+        nc.scalar.activation(warm2[:], warm[:], COPY)
+        nc.gpsimd.dma_start(gain[:], gn.rearrange("(p t) o -> p (t o)", t=PACK))
+        load_scales(nc.gpsimd, w2s, w2_scales)
+
+        sg = tile("sg", [P, S], U8)
+        sm = tile("sm", [P, S], U8)
+        nc.vector.tensor_copy(sg[:], xs[:].indirect(offs_t[:]))
+        nc.vector.tensor_copy(sm[:].bitcast(I32), sg[:].bitcast(I32))
+        for j in range(1, 4):
+            nc.scalar.dma_start(sm[j : P : 32, :].bitcast(I32), sg[8 * j : P : 32, :].bitcast(I32))
+
+        def deal(name, words, scales):
+            dealt_w = tile(name + "_w", [P, PACK, P], I32)
+            dealt_s = tile(name + "_s", [P, PACK, P], U8)
+            nc.vector.tensor_copy(dealt_s[:].rearrange("p t m -> p m t"), scales[:].rearrange("p (m t) -> p m t", t=PACK))
+            nc.vector.tensor_copy(dealt_w[:].rearrange("p t m -> p m t"), words[:].rearrange("p (m t) -> p m t", t=PACK))
+            return dealt_w, dealt_s
+
+        xg = tile("xg", [P, S], U32)
+        w1d, w1ds = deal("w1d", w1w, w1s)
+        nc.vector.tensor_copy(xg[:, :HALF], xw[:].indirect(cut(offs_t, 0, HALF)))
+        nc.vector.tensor_copy(xg[:, HALF:], xw[:].indirect(cut(offs_t, HALF, S)))
+        w2d, w2ds = deal("w2d", w2w, w2s)
+
+        def product(out, w, ws, t, codes, scales):
+            nc.tensor.matmul_mx(out, lhsT=w[:, t, :].bitcast(FP8X4), lhsT_scale=ws[:, t, :],
+                                rhs=codes.bitcast(FP8X4), rhs_scale=scales, start=True, stop=True)
+
+        y_win = [tile("y_win%d" % t, [P, S], F32) for t in range(PACK)]
+        y_plain = tile("y_plain", [P, PACK, S], F32)
+        bank_no = 0
+        for t in range(PACK):
+            for lo, hi in ((0, HALF), (HALF, S)) if t == 0 else ((0, S),):
+                bank = ps.tile([P, S], F32, name="ybank", tag="bank%d" % bank_no)
+                bank_no = bank_no + 1
+                product(bank[:, : hi - lo], w1d, w1ds, t, xg[:, lo:hi], sm[:, lo:hi])
+                nc.scalar.activation(y_win[t][:, lo:hi], bank[:, : hi - lo], COPY, scale=gain[:, t : t + 1])
+                nc.scalar.activation(y_plain[:, t, lo:hi], bank[:, : hi - lo], COPY, scale=gain[:, t : t + 1])
+
+        a_plain = tile("a_plain", [P, PACK, S], F32)
+        a_win = [tile("a_win%d" % t, [P, S], F32) for t in range(PACK)]
+        for t in range(PACK):
+            for lo, hi in ((0, HALF), (HALF, S)):
+                nc.vector.tensor_tensor(a_plain[:, t, lo:hi], y_win[t][:].indirect(cut(n1_t, lo, hi)), y_plain[:, t, lo:hi], ALU.subtract)
+            nc.scalar.activation(a_win[t][:], a_plain[:, t, :], COPY, scale=0.5)
+
+        def weave(engine_copy, name, src, width):
+            woven = tile(name, [P, width, PACK], BF16)
+            engine_copy(woven[:].rearrange("p (c i) t -> p c t i", i=4), src.rearrange("p t (c i) -> p c t i", i=4))
+            return woven
+
+        h_win = [tile("h_win%d" % t, [P, S], F32) for t in range(PACK)]
+        h_plain = tile("h_plain", [P, PACK, S], F32)
+
+        def z_gather(c):
+            lo, hi = Z_PIECES[c]
+            z = tile("z%d" % c, [P, PACK, hi - lo], F32)
+            for t in range(PACK):
+                nc.vector.tensor_tensor(z[:, t, :], a_win[t][:].indirect(cut(n1_t, lo, hi)), a_plain[:, t, lo:hi], ALU.subtract)
+            last = c == len(Z_PIECES) - 1
+            return weave(nc.vector.tensor_copy if last else nc.scalar.copy, "zb%d" % c, z[:], hi - lo)
+
+        h_banks = (("bank5", "bank5", "bank6", "bank6"), ("bank7",) * 4, ("bank0", "bank1", "bank2", "bank3"))
+
+        def h_piece(c, woven):
+            lo, hi = Z_PIECES[c]
+            w = hi - lo
+            zq = tile("zq%d" % c, [P, w], U32)
+            zs = tile("zs%d" % c, [P, w], U8)
+            nc.vector.quantize_mx(zq[:].bitcast(FP8X4), zs[:], woven[:].rearrange("p j t -> p (j t)"))
+            tags = h_banks[c]
+            for tag in sorted(set(tags)):
+                ts = [t for t in range(PACK) if tags[t] == tag]
+                bank = ps.tile([P, len(ts), w], F32, name="hbank", tag=tag)
+                for i, t in enumerate(ts):
+                    product(bank[:, i, :], w2d, w2ds, t, zq[:], zs[:])
+                for i, t in enumerate(ts):
+                    nc.scalar.copy(h_win[t][:, lo:hi], bank[:, i, :])
+                nc.scalar.copy(h_plain[:, ts[0] : ts[-1] + 1, lo:hi], bank[:])
+
+        woven_prev = z_gather(0)
+        for c in range(1, len(Z_PIECES)):
+            woven_next = z_gather(c)
+            h_piece(c - 1, woven_prev)
+            woven_prev = woven_next
+        h_piece(len(Z_PIECES) - 1, woven_prev)
+
+        oq = tile("oq", [P, S], U32)
+        osc = tile("osc", [P, S], U8)
+        out_rows = out_0.rearrange("(p t) j -> p t j", t=PACK)
+        out_words = out_1[0].rearrange("p n t -> p (n t)").bitcast(I32)
+
+        def gathers(c):
+            lo, hi = OUT_PIECES[c]
+            d = tile("d%d" % c, [P, PACK, hi - lo], F32)
+            e = tile("e%d" % c, [P, PACK, hi - lo], F32)
+            steps = []
+            for t in range(PACK):
+                for dst, lists in ((d, n2_t), (e, n3_t)):
+                    steps.append(lambda t=t, dst=dst, lists=lists: nc.vector.tensor_tensor(
+                        dst[:, t, :], h_win[t][:].indirect(cut(lists, lo, hi)), h_plain[:, t, lo:hi], ALU.subtract))
+            return d, e, steps
+
+        def median(c, d, e, t0, t1, res):
+            lo, hi = OUT_PIECES[c]
+            w = hi - lo
+            upper = tile("upper%d_%d" % (c, t0), [P, t1 - t0, w], F32)
+            mid = tile("mid%d_%d" % (c, t0), [P, t1 - t0, w], F32)
+            return [
+                lambda: nc.vector.scalar_tensor_tensor(upper[:], d[:, t0:t1, :], 0.0, e[:, t0:t1, :], ALU.max, ALU.min),
+                lambda: nc.vector.scalar_tensor_tensor(mid[:], d[:, t0:t1, :], 0.0, upper[:], ALU.min, ALU.max),
+                lambda: nc.vector.tensor_tensor(res[:, t0:t1, :], mid[:], h_plain[:, t0:t1, lo:hi], ALU.add),
+            ]
+
+        def hand_out(c, res, engine_copy):
+            lo, hi = OUT_PIECES[c]
+            nc.sync.dma_start(out_rows[:, :, lo:hi], res[:])
+            return weave(engine_copy, "ob%d" % c, res[:], hi - lo)
+
+        def planes(c, woven):
+            lo, hi = OUT_PIECES[c]
+            nc.vector.quantize_mx(oq[:, lo:hi].bitcast(FP8X4), osc[:, lo:hi], woven[:].rearrange("p j t -> p (j t)"))
+            nc.sync.dma_start(out_words[:, lo:hi], oq[:, lo:hi].bitcast(I32))
+
+        pieces = len(OUT_PIECES)
+        res = [tile("res%d" % c, [P, PACK, hi - lo], F32) for c, (lo, hi) in enumerate(OUT_PIECES)]
+        waiting = []
+        woven = {}
+        for c in range(pieces):
+            d, e, steps = gathers(c)
+            for step in steps:
+                step()
+                if waiting:
+                    waiting.pop(0)()
+            first = median(c, d, e, 0, 2, res[c])
+            second = median(c, d, e, 2, 4, res[c])
+            waiting = [op for pair in zip(first, second) for op in pair]
+            if c >= 1:
+                woven[c - 1] = hand_out(c - 1, res[c - 1], nc.scalar.copy)
+            if c >= 2:
+                planes(c - 2, woven[c - 2])
+        for op in waiting:
+            op()
+        planes(pieces - 2, woven[pieces - 2])
+        woven[pieces - 1] = hand_out(pieces - 1, res[pieces - 1], nc.vector.tensor_copy)
+        planes(pieces - 1, woven[pieces - 1])
+        for q in range(4):
+            queue = nc.scalar if q % 2 == 0 else nc.sync
+            queue.dma_start(out_2[0, 4 * q : 4 * q + 4, :].bitcast(I32), osc[32 * q : 32 * q + 4, :].bitcast(I32))

@@ -1,6 +1,7 @@
 from contextlib import ExitStack
 
 import concourse.mybir as mybir
+from concourse.masks import make_identity
 
 K, T, S, N, H = 512, 2048, 512, 512, 512
 FLOPS = 2 * K * H * S + 2 * H * N * S
@@ -38,8 +39,8 @@ def tile_picked_hashtwicemed_none_po_kernel(
         sb = ctx.enter_context(tc.tile_pool(name="sb", bufs=1))
         ps = ctx.enter_context(tc.psum_pool(name="ps", bufs=1))
 
-        def tile(name, shape, dtype):
-            return sb.tile(shape, dtype, name=name, align_bytes=64)
+        def tile(name, shape, dtype, tag=""):
+            return sb.tile(shape, dtype, name=name, tag=tag or name, align_bytes=64)
 
         offs_t = tile("offs_t", [P, S // GROUP], U16)
         n1_t = tile("n1_t", [P, S // GROUP], U16)
@@ -68,12 +69,12 @@ def tile_picked_hashtwicemed_none_po_kernel(
         nc.sync.dma_start(w1w[:], words_of(w1_words))
         nc.sync.dma_start(xw[:].bitcast(I32), words_of(x_words))
         nc.sync.dma_start(n1_t[:], n1)
+        load_scales(nc.sync, w2s, w2_scales)
+        nc.sync.dma_start(w2w[:], words_of(w2_words))
         nc.sync.dma_start(n2_t[:], n2)
         nc.sync.dma_start(n3_t[:], n3)
-        nc.sync.dma_start(w2w[:], words_of(w2_words))
         nc.scalar.activation(warm2[:], warm[:], COPY)
         nc.gpsimd.dma_start(gain[:], gn.rearrange("(p t) o -> p (t o)", t=PACK))
-        load_scales(nc.gpsimd, w2s, w2_scales)
 
         sg = tile("sg", [P, S], U8)
         sm = tile("sm", [P, S], U8)
@@ -99,8 +100,12 @@ def tile_picked_hashtwicemed_none_po_kernel(
             nc.tensor.matmul_mx(out, lhsT=w[:, t, :].bitcast(FP8X4), lhsT_scale=ws[:, t, :],
                                 rhs=codes.bitcast(FP8X4), rhs_scale=scales, start=True, stop=True)
 
-        y_win = [tile("y_win%d" % t, [P, S], F32) for t in range(PACK)]
-        y_plain = tile("y_plain", [P, PACK, S], F32)
+        ident = tile("ident", [P, P], F32)
+        make_identity(nc, ident[:])
+
+        y_win = [tile("y_win%d" % t, [P, S if t == 0 else 2 * S], F32) for t in range(PACK)]
+        y_last = tile("y_last", [P, S], F32)
+        y_plain = [y_win[t + 1][:, S:] for t in range(PACK - 1)] + [y_last[:]]
         bank_no = 0
         for t in range(PACK):
             for lo, hi in ((0, HALF), (HALF, S)) if t == 0 else ((0, S),):
@@ -108,32 +113,31 @@ def tile_picked_hashtwicemed_none_po_kernel(
                 bank_no = bank_no + 1
                 product(bank[:, : hi - lo], w1d, w1ds, t, xg[:, lo:hi], sm[:, lo:hi])
                 nc.scalar.activation(y_win[t][:, lo:hi], bank[:, : hi - lo], COPY, scale=gain[:, t : t + 1])
-                nc.scalar.activation(y_plain[:, t, lo:hi], bank[:, : hi - lo], COPY, scale=gain[:, t : t + 1])
+                nc.scalar.activation(y_plain[t][:, lo:hi], bank[:, : hi - lo], COPY, scale=gain[:, t : t + 1])
 
-        a_plain = tile("a_plain", [P, PACK, S], F32)
+        h_win = [tile("h_win%d" % t, [P, S if t == PACK - 1 else 2 * S], F32) for t in range(PACK)]
+        a_last = tile("a_last", [P, S], F32)
+        a_plain = [h_win[t][:, S:] for t in range(PACK - 1)] + [a_last[:]]
         a_win = [tile("a_win%d" % t, [P, S], F32) for t in range(PACK)]
         for t in range(PACK):
-            for lo, hi in ((0, HALF), (HALF, S)):
-                nc.vector.tensor_tensor(a_plain[:, t, lo:hi], y_win[t][:].indirect(cut(n1_t, lo, hi)), y_plain[:, t, lo:hi], ALU.subtract)
-            nc.scalar.activation(a_win[t][:], a_plain[:, t, :], COPY, scale=0.5)
+            for lo, hi in ((0, HALF), (HALF, S)) if t == 0 else ((0, S),):
+                nc.vector.tensor_tensor(a_plain[t][:, lo:hi], y_win[t][:].indirect(cut(n1_t, lo, hi)), y_plain[t][:, lo:hi], ALU.subtract)
+            nc.scalar.activation(a_win[t][:], a_plain[t], COPY, scale=0.5)
 
-        def weave(engine_copy, name, src, width):
-            woven = tile(name, [P, width, PACK], BF16)
-            engine_copy(woven[:].rearrange("p (c i) t -> p c t i", i=4), src.rearrange("p t (c i) -> p c t i", i=4))
-            return woven
+        def weave_pair(engine_copy, woven, u, src):
+            engine_copy(woven[:, :, 2 * u : 2 * u + 2], src.rearrange("p t j -> p j t"))
 
-        h_win = [tile("h_win%d" % t, [P, S], F32) for t in range(PACK)]
         h_plain = tile("h_plain", [P, PACK, S], F32)
 
-        def z_gather(c):
+        def z_gather(c, u, tag=""):
             lo, hi = Z_PIECES[c]
-            z = tile("z%d" % c, [P, PACK, hi - lo], F32)
-            for t in range(PACK):
-                nc.vector.tensor_tensor(z[:, t, :], a_win[t][:].indirect(cut(n1_t, lo, hi)), a_plain[:, t, lo:hi], ALU.subtract)
-            last = c == len(Z_PIECES) - 1
-            return weave(nc.vector.tensor_copy if last else nc.scalar.copy, "zb%d" % c, z[:], hi - lo)
+            z = tile("z%d_%d" % (c, u), [P, 2, hi - lo], F32, tag)
+            for i in range(2):
+                t = 2 * u + i
+                nc.vector.tensor_tensor(z[:, i, :], a_win[t][:].indirect(cut(n1_t, lo, hi)), a_plain[t][:, lo:hi], ALU.subtract)
+            return z[:]
 
-        h_banks = (("bank5", "bank5", "bank6", "bank6"), ("bank7",) * 4, ("bank0", "bank1", "bank2", "bank3"))
+        h_banks = [None] + [ps.tile([P, S], F32, name="hbank", tag="bank%d" % (2 + t)) for t in range(1, PACK)]
 
         def h_piece(c, woven):
             lo, hi = Z_PIECES[c]
@@ -141,82 +145,120 @@ def tile_picked_hashtwicemed_none_po_kernel(
             zq = tile("zq%d" % c, [P, w], U32)
             zs = tile("zs%d" % c, [P, w], U8)
             nc.vector.quantize_mx(zq[:].bitcast(FP8X4), zs[:], woven[:].rearrange("p j t -> p (j t)"))
-            tags = h_banks[c]
-            for tag in sorted(set(tags)):
-                ts = [t for t in range(PACK) if tags[t] == tag]
-                bank = ps.tile([P, len(ts), w], F32, name="hbank", tag=tag)
-                for i, t in enumerate(ts):
-                    product(bank[:, i, :], w2d, w2ds, t, zq[:], zs[:])
-                for i, t in enumerate(ts):
-                    nc.scalar.copy(h_win[t][:, lo:hi], bank[:, i, :])
-                nc.scalar.copy(h_plain[:, ts[0] : ts[-1] + 1, lo:hi], bank[:])
+            first = ps.tile([P, w], F32, name="hfirst", tag="bank%d" % c)
+            product(first[:], w2d, w2ds, 0, zq[:], zs[:])
+            nc.scalar.copy(h_win[0][:, lo:hi], first[:])
+            nc.scalar.copy(h_plain[:, 0, lo:hi], first[:])
+            for t in range(1, PACK):
+                product(h_banks[t][:, lo:hi], w2d, w2ds, t, zq[:], zs[:])
 
-        woven_prev = z_gather(0)
-        for c in range(1, len(Z_PIECES)):
-            woven_next = z_gather(c)
-            h_piece(c - 1, woven_prev)
-            woven_prev = woven_next
-        h_piece(len(Z_PIECES) - 1, woven_prev)
+        zb = [tile("zb%d" % c, [P, hi - lo, PACK], BF16) for c, (lo, hi) in enumerate(Z_PIECES)]
+        for c in range(2):
+            for u in range(2):
+                weave_pair(nc.scalar.copy, zb[c], u, z_gather(c, u))
+        h_piece(0, zb[0])
+        weave_pair(nc.scalar.copy, zb[2], 0, z_gather(2, 0, "zb0"))
+        h_piece(1, zb[1])
+        weave_pair(nc.vector.tensor_copy, zb[2], 1, z_gather(2, 1, "zb1"))
+        h_piece(2, zb[2])
+        for t in range(1, PACK):
+            nc.scalar.copy(h_win[t][:, :S], h_banks[t][:])
+            nc.scalar.copy(h_plain[:, t, :], h_banks[t][:])
 
         oq = tile("oq", [P, S], U32)
         osc = tile("osc", [P, S], U8)
         out_rows = out_0.rearrange("(p t) j -> p t j", t=PACK)
         out_words = out_1[0].rearrange("p n t -> p (n t)").bitcast(I32)
 
-        def gathers(c):
-            lo, hi = OUT_PIECES[c]
-            d = tile("d%d" % c, [P, PACK, hi - lo], F32)
-            e = tile("e%d" % c, [P, PACK, hi - lo], F32)
-            steps = []
-            for t in range(PACK):
-                for dst, lists in ((d, n2_t), (e, n3_t)):
-                    steps.append(lambda t=t, dst=dst, lists=lists: nc.vector.tensor_tensor(
-                        dst[:, t, :], h_win[t][:].indirect(cut(lists, lo, hi)), h_plain[:, t, lo:hi], ALU.subtract))
-            return d, e, steps
+        res = tile("res", [P, PACK, S], F32)
+        d = [tile("d%d" % i, [P, S], F32) for i in range(2)]
+        e = [tile("e%d" % i, [P, S], F32) for i in range(2)]
+        upper = tile("upper", [P, PACK, S], F32)
+        mid = tile("mid", [P, PACK, S], F32)
 
-        def median(c, d, e, t0, t1, res):
-            lo, hi = OUT_PIECES[c]
-            w = hi - lo
-            upper = tile("upper%d_%d" % (c, t0), [P, t1 - t0, w], F32)
-            mid = tile("mid%d_%d" % (c, t0), [P, t1 - t0, w], F32)
-            return [
-                lambda: nc.vector.scalar_tensor_tensor(upper[:], d[:, t0:t1, :], 0.0, e[:, t0:t1, :], ALU.max, ALU.min),
-                lambda: nc.vector.scalar_tensor_tensor(mid[:], d[:, t0:t1, :], 0.0, upper[:], ALU.min, ALU.max),
-                lambda: nc.vector.tensor_tensor(res[:, t0:t1, :], mid[:], h_plain[:, t0:t1, lo:hi], ALU.add),
-            ]
+        def fetch(dst, lists, t, lo, hi):
+            nc.vector.tensor_tensor(dst, h_win[t][:].indirect(cut(lists, lo, hi)), h_plain[:, t, lo:hi], ALU.subtract)
 
-        def hand_out(c, res, engine_copy):
-            lo, hi = OUT_PIECES[c]
-            nc.sync.dma_start(out_rows[:, :, lo:hi], res[:])
-            return weave(engine_copy, "ob%d" % c, res[:], hi - lo)
+        def fetch_pair(i, t, lo, hi):
+            fetch(d[i][:, : hi - lo], n2_t, t, lo, hi)
+            fetch(e[i][:, : hi - lo], n3_t, t, lo, hi)
+
+        def op1(i, t, lo, hi):
+            nc.vector.scalar_tensor_tensor(upper[:, t, lo:hi], d[i][:, : hi - lo], 0.0, e[i][:, : hi - lo], ALU.max, ALU.min)
+
+        def op2(i, t, lo, hi):
+            nc.vector.scalar_tensor_tensor(mid[:, t, lo:hi], d[i][:, : hi - lo], 0.0, upper[:, t, lo:hi], ALU.min, ALU.max)
+
+        def op3(t, lo, hi):
+            nc.vector.tensor_tensor(res[:, t, lo:hi], mid[:, t, lo:hi], h_plain[:, t, lo:hi], ALU.add)
+
+        def store(t, lo, hi):
+            nc.sync.dma_start(out_rows[:, t, lo:hi], res[:, t, lo:hi])
+
+        def op3_tensor(t):
+            there = ps.tile([P, PACK, P], F32, name="there", tag="bank%d" % (6 + t))
+            back = ps.tile([P, PACK, P], F32, name="back", tag="bank%d" % t)
+            turned = tile("turned%d" % t, [P, PACK, P], F32)
+            for b in range(PACK):
+                cols = slice(b * P, (b + 1) * P)
+                nc.tensor.matmul(there[:, b, :], h_plain[:, t, cols], ident[:], start=True, stop=False, is_transpose=True)
+                nc.tensor.matmul(there[:, b, :], mid[:, t, cols], ident[:], start=False, stop=True, is_transpose=True)
+            nc.scalar.copy(turned[:], there[:])
+            for b in range(PACK):
+                nc.tensor.transpose(back[:, b, :], turned[:, b, :], ident[:])
+            nc.scalar.copy(res[:, t, :], back[:].rearrange("p b j -> p (b j)"))
+            nc.sync.dma_start(out_rows[:, t, :], res[:, t, :])
 
         def planes(c, woven):
             lo, hi = OUT_PIECES[c]
             nc.vector.quantize_mx(oq[:, lo:hi].bitcast(FP8X4), osc[:, lo:hi], woven[:].rearrange("p j t -> p (j t)"))
+
+        def store_words(lo, hi):
             nc.sync.dma_start(out_words[:, lo:hi], oq[:, lo:hi].bitcast(I32))
 
-        pieces = len(OUT_PIECES)
-        res = [tile("res%d" % c, [P, PACK, hi - lo], F32) for c, (lo, hi) in enumerate(OUT_PIECES)]
-        waiting = []
-        woven = {}
-        for c in range(pieces):
-            d, e, steps = gathers(c)
-            for step in steps:
-                step()
-                if waiting:
-                    waiting.pop(0)()
-            first = median(c, d, e, 0, 2, res[c])
-            second = median(c, d, e, 2, 4, res[c])
-            waiting = [op for pair in zip(first, second) for op in pair]
-            if c >= 1:
-                woven[c - 1] = hand_out(c - 1, res[c - 1], nc.scalar.copy)
-            if c >= 2:
-                planes(c - 2, woven[c - 2])
-        for op in waiting:
-            op()
-        planes(pieces - 2, woven[pieces - 2])
-        woven[pieces - 1] = hand_out(pieces - 1, res[pieces - 1], nc.vector.tensor_copy)
-        planes(pieces - 1, woven[pieces - 1])
+        ob = [tile("ob%d" % c, [P, hi - lo, PACK], BF16) for c, (lo, hi) in enumerate(OUT_PIECES)]
+
+        def hand(c, u, engine_copy):
+            lo, hi = OUT_PIECES[c]
+            weave_pair(engine_copy, ob[c], u, res[:, 2 * u : 2 * u + 2, lo:hi])
+
+        p0, p1, p2 = OUT_PIECES
+        fetch(d[0][:, :HALF], n2_t, 0, 0, HALF)
+        fetch(d[0][:, HALF:], n2_t, 0, HALF, S)
+        fetch(e[0][:], n3_t, 0, 0, S)
+        fetch_pair(1, 1, 0, S)
+        for op in (op1, op2):
+            op(0, 0, 0, S)
+            op(1, 1, 0, S)
+        op3_tensor(0)
+        op3_tensor(1)
+        for c in range(3):
+            hand(c, 0, nc.scalar.copy)
+        fetch_pair(0, 2, 0, S)
+        fetch_pair(1, 3, *p0)
+        for op in (op1, op2):
+            op(0, 2, 0, S)
+            op(1, 3, *p0)
+        op3(2, 0, S)
+        store(2, 0, S)
+        op3(3, *p0)
+        store(3, *p0)
+        hand(0, 1, nc.scalar.copy)
+        fetch_pair(0, 3, *p1)
+        fetch_pair(1, 3, *p2)
+        for op in (op1, op2):
+            op(0, 3, *p1)
+            op(1, 3, *p2)
+        planes(0, ob[0])
+        store_words(*p0)
+        op3(3, *p1)
+        op3(3, *p2)
+        store(3, p1[0], S)
+        hand(1, 1, nc.vector.tensor_copy)
+        hand(2, 1, nc.vector.tensor_copy)
+        planes(1, ob[1])
+        planes(2, ob[2])
+        store_words(p1[0], S)
         for q in range(4):
-            queue = nc.scalar if q % 2 == 0 else nc.sync
+            queue = nc.sync if q == 3 else nc.scalar
             queue.dma_start(out_2[0, 4 * q : 4 * q + 4, :].bitcast(I32), osc[32 * q : 32 * q + 4, :].bitcast(I32))

from contextlib import ExitStack

import concourse.mybir as mybir
from concourse.masks import make_identity

K, T, S, N, H = 512, 2048, 512, 512, 512
FLOPS = 2 * K * H * S + 2 * H * N * S

F32 = mybir.dt.float32
BF16 = mybir.dt.bfloat16
I32 = mybir.dt.int32
U32 = mybir.dt.uint32
U16 = mybir.dt.uint16
U8 = mybir.dt.uint8
FP8X4 = mybir.dt.float8_e4m3fn_x4
ALU = mybir.AluOpType
COPY = mybir.ActivationFunctionType.Copy

P = 128
PACK = 4
GROUP = 16
HALF = S // 2
Z_PIECES = ((0, 256), (256, 384), (384, 512))
OUT_PIECES = ((0, 256), (256, 384), (384, 512))


def tile_picked_hashtwicemed_none_po_kernel(
    tc, x_words, x_scales, w1_words, w1_scales, gn, w2_words, w2_scales, offs, n1, n2, n3, out_0, out_1, out_2
):
    nc = tc.nc

    def words_of(dram):
        return dram[0].rearrange("p n t -> p (n t)").bitcast(I32)

    def cut(lists, lo, hi):
        return lists[:, lo // GROUP : hi // GROUP]

    with ExitStack() as ctx:
        sb = ctx.enter_context(tc.tile_pool(name="sb", bufs=1))
        ps = ctx.enter_context(tc.psum_pool(name="ps", bufs=1))

        def tile(name, shape, dtype, tag=""):
            return sb.tile(shape, dtype, name=name, tag=tag or name, align_bytes=64)

        offs_t = tile("offs_t", [P, S // GROUP], U16)
        n1_t = tile("n1_t", [P, S // GROUP], U16)
        n2_t = tile("n2_t", [P, S // GROUP], U16)
        n3_t = tile("n3_t", [P, S // GROUP], U16)
        xw = tile("xw", [P, T], U32)
        xs = tile("xs", [P, T], U8)
        w1w = tile("w1w", [P, H], I32)
        w2w = tile("w2w", [P, N], I32)
        w1s = tile("w1s", [P, H], U8)
        w2s = tile("w2s", [P, N], U8)
        gain = tile("gain", [P, PACK], F32)
        warm = tile("warm", [P, 8], F32)
        warm2 = tile("warm2", [P, 8], F32)

        nc.vector.memset(warm[:], 0.0)

        def load_scales(queue, dst, src):
            for q in range(4):
                rows = src[0, 4 * q : 4 * q + 4, :].bitcast(I32)
                queue.dma_start(dst[32 * q : 32 * q + 32, :].bitcast(I32), rows.partition_broadcast(8))

        nc.sync.dma_start(offs_t[:], offs)
        nc.sync.dma_start(xs[:].bitcast(I32), x_scales[0].bitcast(I32).unsqueeze(1).to_broadcast([16, 8, T // 4]))
        load_scales(nc.sync, w1s, w1_scales)
        nc.sync.dma_start(w1w[:], words_of(w1_words))
        nc.sync.dma_start(xw[:].bitcast(I32), words_of(x_words))
        nc.sync.dma_start(n1_t[:], n1)
        load_scales(nc.sync, w2s, w2_scales)
        nc.sync.dma_start(w2w[:], words_of(w2_words))
        nc.sync.dma_start(n2_t[:], n2)
        nc.sync.dma_start(n3_t[:], n3)
        nc.scalar.activation(warm2[:], warm[:], COPY)
        nc.gpsimd.dma_start(gain[:], gn.rearrange("(p t) o -> p (t o)", t=PACK))

        sg = tile("sg", [P, S], U8)
        sm = tile("sm", [P, S], U8)
        nc.vector.tensor_copy(sg[:], xs[:].indirect(offs_t[:]))
        nc.vector.tensor_copy(sm[:].bitcast(I32), sg[:].bitcast(I32))
        for j in range(1, 4):
            nc.scalar.dma_start(sm[j : P : 32, :].bitcast(I32), sg[8 * j : P : 32, :].bitcast(I32))

        def deal(name, words, scales):
            dealt_w = tile(name + "_w", [P, PACK, P], I32)
            dealt_s = tile(name + "_s", [P, PACK, P], U8)
            nc.vector.tensor_copy(dealt_s[:].rearrange("p t m -> p m t"), scales[:].rearrange("p (m t) -> p m t", t=PACK))
            nc.vector.tensor_copy(dealt_w[:].rearrange("p t m -> p m t"), words[:].rearrange("p (m t) -> p m t", t=PACK))
            return dealt_w, dealt_s

        xg = tile("xg", [P, S], U32)
        w1d, w1ds = deal("w1d", w1w, w1s)
        nc.vector.tensor_copy(xg[:, :HALF], xw[:].indirect(cut(offs_t, 0, HALF)))
        nc.vector.tensor_copy(xg[:, HALF:], xw[:].indirect(cut(offs_t, HALF, S)))
        w2d, w2ds = deal("w2d", w2w, w2s)

        def product(out, w, ws, t, codes, scales):
            nc.tensor.matmul_mx(out, lhsT=w[:, t, :].bitcast(FP8X4), lhsT_scale=ws[:, t, :],
                                rhs=codes.bitcast(FP8X4), rhs_scale=scales, start=True, stop=True)

        ident = tile("ident", [P, P], F32)
        make_identity(nc, ident[:])

        y_win = [tile("y_win%d" % t, [P, S if t == 0 else 2 * S], F32) for t in range(PACK)]
        y_last = tile("y_last", [P, S], F32)
        y_plain = [y_win[t + 1][:, S:] for t in range(PACK - 1)] + [y_last[:]]
        bank_no = 0
        for t in range(PACK):
            for lo, hi in ((0, HALF), (HALF, S)) if t == 0 else ((0, S),):
                bank = ps.tile([P, S], F32, name="ybank", tag="bank%d" % bank_no)
                bank_no = bank_no + 1
                product(bank[:, : hi - lo], w1d, w1ds, t, xg[:, lo:hi], sm[:, lo:hi])
                nc.scalar.activation(y_win[t][:, lo:hi], bank[:, : hi - lo], COPY, scale=gain[:, t : t + 1])
                nc.scalar.activation(y_plain[t][:, lo:hi], bank[:, : hi - lo], COPY, scale=gain[:, t : t + 1])

        h_win = [tile("h_win%d" % t, [P, S if t == PACK - 1 else 2 * S], F32) for t in range(PACK)]
        a_last = tile("a_last", [P, S], F32)
        a_plain = [h_win[t][:, S:] for t in range(PACK - 1)] + [a_last[:]]
        a_win = [tile("a_win%d" % t, [P, S], F32) for t in range(PACK)]
        for t in range(PACK):
            for lo, hi in ((0, HALF), (HALF, S)) if t == 0 else ((0, S),):
                nc.vector.tensor_tensor(a_plain[t][:, lo:hi], y_win[t][:].indirect(cut(n1_t, lo, hi)), y_plain[t][:, lo:hi], ALU.subtract)
            nc.scalar.activation(a_win[t][:], a_plain[t], COPY, scale=0.5)

        def weave_pair(engine_copy, woven, u, src):
            engine_copy(woven[:, :, 2 * u : 2 * u + 2], src.rearrange("p t j -> p j t"))

        h_plain = tile("h_plain", [P, PACK, S], F32)

        def z_gather(c, u, tag=""):
            lo, hi = Z_PIECES[c]
            z = tile("z%d_%d" % (c, u), [P, 2, hi - lo], F32, tag)
            for i in range(2):
                t = 2 * u + i
                nc.vector.tensor_tensor(z[:, i, :], a_win[t][:].indirect(cut(n1_t, lo, hi)), a_plain[t][:, lo:hi], ALU.subtract)
            return z[:]

        h_banks = [None] + [ps.tile([P, S], F32, name="hbank", tag="bank%d" % (2 + t)) for t in range(1, PACK)]

        def h_piece(c, woven):
            lo, hi = Z_PIECES[c]
            w = hi - lo
            zq = tile("zq%d" % c, [P, w], U32)
            zs = tile("zs%d" % c, [P, w], U8)
            nc.vector.quantize_mx(zq[:].bitcast(FP8X4), zs[:], woven[:].rearrange("p j t -> p (j t)"))
            first = ps.tile([P, w], F32, name="hfirst", tag="bank%d" % c)
            product(first[:], w2d, w2ds, 0, zq[:], zs[:])
            nc.scalar.copy(h_win[0][:, lo:hi], first[:])
            nc.scalar.copy(h_plain[:, 0, lo:hi], first[:])
            for t in range(1, PACK):
                product(h_banks[t][:, lo:hi], w2d, w2ds, t, zq[:], zs[:])

        zb = [tile("zb%d" % c, [P, hi - lo, PACK], BF16) for c, (lo, hi) in enumerate(Z_PIECES)]
        for c in range(2):
            for u in range(2):
                weave_pair(nc.scalar.copy, zb[c], u, z_gather(c, u))
        h_piece(0, zb[0])
        weave_pair(nc.scalar.copy, zb[2], 0, z_gather(2, 0, "zb0"))
        h_piece(1, zb[1])
        weave_pair(nc.vector.tensor_copy, zb[2], 1, z_gather(2, 1, "zb1"))
        h_piece(2, zb[2])
        for t in range(1, PACK):
            nc.scalar.copy(h_win[t][:, :S], h_banks[t][:])
            nc.scalar.copy(h_plain[:, t, :], h_banks[t][:])

        oq = tile("oq", [P, S], U32)
        osc = tile("osc", [P, S], U8)
        out_rows = out_0.rearrange("(p t) j -> p t j", t=PACK)
        out_words = out_1[0].rearrange("p n t -> p (n t)").bitcast(I32)

        res = tile("res", [P, PACK, S], F32)
        d = [tile("d%d" % i, [P, S], F32) for i in range(2)]
        e = [tile("e%d" % i, [P, S], F32) for i in range(2)]
        upper = tile("upper", [P, PACK, S], F32)
        mid = tile("mid", [P, PACK, S], F32)

        def fetch(dst, lists, t, lo, hi):
            nc.vector.tensor_tensor(dst, h_win[t][:].indirect(cut(lists, lo, hi)), h_plain[:, t, lo:hi], ALU.subtract)

        def fetch_pair(i, t, lo, hi):
            fetch(d[i][:, : hi - lo], n2_t, t, lo, hi)
            fetch(e[i][:, : hi - lo], n3_t, t, lo, hi)

        def op1(i, t, lo, hi):
            nc.vector.scalar_tensor_tensor(upper[:, t, lo:hi], d[i][:, : hi - lo], 0.0, e[i][:, : hi - lo], ALU.max, ALU.min)

        def op2(i, t, lo, hi):
            nc.vector.scalar_tensor_tensor(mid[:, t, lo:hi], d[i][:, : hi - lo], 0.0, upper[:, t, lo:hi], ALU.min, ALU.max)

        def op3(t, lo, hi):
            nc.vector.tensor_tensor(res[:, t, lo:hi], mid[:, t, lo:hi], h_plain[:, t, lo:hi], ALU.add)

        def store(t, lo, hi):
            nc.sync.dma_start(out_rows[:, t, lo:hi], res[:, t, lo:hi])

        def op3_tensor(t):
            there = ps.tile([P, PACK, P], F32, name="there", tag="bank%d" % (6 + t))
            back = ps.tile([P, PACK, P], F32, name="back", tag="bank%d" % t)
            turned = tile("turned%d" % t, [P, PACK, P], F32)
            for b in range(PACK):
                cols = slice(b * P, (b + 1) * P)
                nc.tensor.matmul(there[:, b, :], h_plain[:, t, cols], ident[:], start=True, stop=False, is_transpose=True)
                nc.tensor.matmul(there[:, b, :], mid[:, t, cols], ident[:], start=False, stop=True, is_transpose=True)
            nc.scalar.copy(turned[:], there[:])
            for b in range(PACK):
                nc.tensor.transpose(back[:, b, :], turned[:, b, :], ident[:])
            nc.scalar.copy(res[:, t, :], back[:].rearrange("p b j -> p (b j)"))
            nc.sync.dma_start(out_rows[:, t, :], res[:, t, :])

        def planes(c, woven):
            lo, hi = OUT_PIECES[c]
            nc.vector.quantize_mx(oq[:, lo:hi].bitcast(FP8X4), osc[:, lo:hi], woven[:].rearrange("p j t -> p (j t)"))

        def store_words(lo, hi):
            nc.sync.dma_start(out_words[:, lo:hi], oq[:, lo:hi].bitcast(I32))

        ob = [tile("ob%d" % c, [P, hi - lo, PACK], BF16) for c, (lo, hi) in enumerate(OUT_PIECES)]

        def hand(c, u, engine_copy):
            lo, hi = OUT_PIECES[c]
            weave_pair(engine_copy, ob[c], u, res[:, 2 * u : 2 * u + 2, lo:hi])

        p0, p1, p2 = OUT_PIECES
        fetch(d[0][:, :HALF], n2_t, 0, 0, HALF)
        fetch(d[0][:, HALF:], n2_t, 0, HALF, S)
        fetch(e[0][:], n3_t, 0, 0, S)
        fetch_pair(1, 1, 0, S)
        for op in (op1, op2):
            op(0, 0, 0, S)
            op(1, 1, 0, S)
        op3_tensor(0)
        op3_tensor(1)
        for c in range(3):
            hand(c, 0, nc.scalar.copy)
        fetch_pair(0, 2, 0, S)
        fetch_pair(1, 3, *p0)
        for op in (op1, op2):
            op(0, 2, 0, S)
            op(1, 3, *p0)
        op3(2, 0, S)
        store(2, 0, S)
        op3(3, *p0)
        store(3, *p0)
        hand(0, 1, nc.scalar.copy)
        fetch_pair(0, 3, *p1)
        fetch_pair(1, 3, *p2)
        for op in (op1, op2):
            op(0, 3, *p1)
            op(1, 3, *p2)
        planes(0, ob[0])
        store_words(*p0)
        op3(3, *p1)
        op3(3, *p2)
        store(3, p1[0], S)
        hand(1, 1, nc.vector.tensor_copy)
        hand(2, 1, nc.vector.tensor_copy)
        planes(1, ob[1])
        planes(2, ob[2])
        store_words(p1[0], S)
        for q in range(4):
            queue = nc.sync if q == 3 else nc.scalar
            queue.dma_start(out_2[0, 4 * q : 4 * q + 4, :].bitcast(I32), osc[32 * q : 32 * q + 4, :].bitcast(I32))
